import numpy as np
import ml_dtypes


def mxq(x, axis, fmt="e4m3"):
    dtype, down = {"e4m3": (ml_dtypes.float8_e4m3fn, 7), "e5m2": (ml_dtypes.float8_e5m2, 14)}[fmt]
    v = np.moveaxis(np.asarray(x, np.float32).astype(ml_dtypes.bfloat16).astype(np.float64), axis, -1)
    blocks = v.reshape(v.shape[:-1] + (-1, 32))
    amax = np.abs(blocks).max(-1, keepdims=True)
    byte = np.maximum(np.where(amax > 0, np.frexp(amax)[1] - 1 + 127, 0) - down, 1)
    scale = np.exp2(byte - 127.0)
    codes = (blocks / scale).astype(np.float32).astype(dtype).astype(np.float64)
    return np.moveaxis((codes * scale).reshape(v.shape), -1, axis)


WIDE = False


def mx_kscale(k):
    if not WIDE:
        return np.ones(k)
    levels = np.array([30, -30])
    if k % 512:
        return np.exp2(np.random.permutation(np.resize(levels, k // 32))).repeat(32)
    a = np.empty((k // 512, 16))
    for p in range(k // 512):
        a[p, :8] = np.random.permutation(np.resize(levels, 8))
        for g in range(8):
            far = levels[np.abs(levels - a[p, g]) >= 10]
            a[p, g + 8] = far[np.random.randint(len(far))]
    return np.exp2(a.ravel()).repeat(32)


def f64(x):
    return np.asarray(x).astype(np.float64)


def striped(idx):
    return np.tile(np.asarray(idx).reshape(-1, 16).T, (8, 1)).astype(np.uint16)


def unstriped(offs):
    return offs[:16].T.reshape(-1).astype(np.int64)


def striped8(idx):
    return np.asarray(idx).reshape(8, -1, 16).transpose(0, 2, 1).reshape(128, -1).astype(np.uint16)


def unstriped8(offs):
    return offs.reshape(8, 16, -1).transpose(0, 2, 1).reshape(8, -1).astype(np.int64)


def pick8(x, idx, run):
    r = np.arange(len(x))
    return x[r[:, None], idx[r % (8 * run) // run]]


E2M1 = np.array([0.0, 0.5, 1.0, 1.5, 2.0, 3.0, 4.0, 6.0, -0.0, -0.5, -1.0, -1.5, -2.0, -3.0, -4.0, -6.0])


def pack_weight(w, fmt):
    k, n = w.shape
    w = f64(np.asarray(w, np.float32).astype(ml_dtypes.bfloat16)).reshape(k // 32, 32, n)
    amax = np.abs(w).max(1)
    if fmt in ("e4m3", "e5m2"):
        byte = np.frexp(amax)[1] - 1 + 127 - (7 if fmt == "e4m3" else 14)
    else:
        mant, ex = np.frexp(amax / 6.0)
        byte = np.where(mant > 0.5, ex, ex - 1) + 127
    byte = np.clip(np.where(amax > 0, byte, 1), 1, 254)
    scaled = (w * np.exp2(127.0 - byte)[:, None, :]).reshape(k, n).astype(np.float32)
    by_word = np.ascontiguousarray(scaled.reshape(k // 512, 128, 4, n).transpose(0, 1, 3, 2))
    if fmt in ("e4m3", "e5m2"):
        words = by_word.astype(ml_dtypes.float8_e4m3fn if fmt == "e4m3" else ml_dtypes.float8_e5m2).view(np.uint8)
    else:
        c = by_word.astype(ml_dtypes.float4_e2m1fn).view(np.uint8) & 0xF
        words = (c[..., 0::2] | (c[..., 1::2] << 4)).reshape(k // 512, 128, 2 * n)
    return np.ascontiguousarray(words), np.ascontiguousarray(byte.astype(np.uint8).reshape(k // 512, 16, n))


def unpack_weight(words, scales, fmt):
    g, _, n = scales.shape
    words = np.ascontiguousarray(words).reshape(g, 128, n, -1)
    if fmt in ("e4m3", "e5m2"):
        vals = words.view(ml_dtypes.float8_e4m3fn if fmt == "e4m3" else ml_dtypes.float8_e5m2).astype(np.float64)
    else:
        nib = np.empty((g, 128, n, 4), np.uint8)
        nib[..., 0::2] = words & 0xF
        nib[..., 1::2] = words >> 4
        vals = E2M1[nib]
    vals = vals * np.repeat(np.exp2(scales.astype(np.float64) - 127.0), 8, axis=1)[..., None]
    return vals.transpose(0, 1, 3, 2).reshape(g * 512, n)


K, T, J, R, F, Z, C, N = 512, 1024, 256, 512, 512, 1024, 512, 256


def setup_inputs():
    n = np.random.standard_normal
    idx = np.random.permutation(T)[:J]
    idx2 = np.random.permutation(Z)[:J]
    idx3 = np.stack([np.random.permutation(C)[:J] for _ in range(8)])
    idx4 = np.stack([np.random.permutation(C)[:J] for _ in range(8)])
    fk = mx_kscale(K)
    ff = mx_kscale(F)
    fr = mx_kscale(R)
    xtp = pack_weight(n((K, T)) / fk[:, None], "e5m2")
    xop = pack_weight(n((F, Z)) / ff[:, None], "e4m3")
    wp = pack_weight(n((K, R)) * 1 / np.sqrt(K) * fk[:, None] * fr, "e2m1")
    w0p = pack_weight(n((F, R)) * 1 / np.sqrt(F) * ff[:, None] * fr, "e2m1")
    w2p = pack_weight(n((F, R)) * 1 / np.sqrt(F) * ff[:, None] * fr, "e4m3")
    wbp = pack_weight(n((R, N)) * 1 / np.sqrt(R) / fr[:, None], "e2m1")
    return {
        "xt_words": xtp[0],
        "xt_scales": xtp[1],
        "xo_words": xop[0],
        "xo_scales": xop[1],
        "w_words": wp[0],
        "w_scales": wp[1],
        "w0_words": w0p[0],
        "w0_scales": w0p[1],
        "w2_words": w2p[0],
        "w2_scales": w2p[1],
        "wb_words": wbp[0],
        "wb_scales": wbp[1],
        "offs": striped(idx),
        "offs2": striped(idx2),
        "offs3": striped8(idx3),
        "offs4": striped8(idx4),
    }


def reference(xt_words, xt_scales, xo_words, xo_scales, w_words, w_scales, w0_words, w0_scales, w2_words, w2_scales, wb_words, wb_scales, offs, offs2, offs3, offs4):
    idx = unstriped(offs)
    idx2 = unstriped(offs2)
    idx3 = unstriped8(offs3)
    idx4 = unstriped8(offs4)
    xtu = unpack_weight(xt_words, xt_scales, "e5m2")
    xou = unpack_weight(xo_words, xo_scales, "e4m3")
    wu = unpack_weight(w_words, w_scales, "e2m1")
    w0u = unpack_weight(w0_words, w0_scales, "e2m1")
    w2u = unpack_weight(w2_words, w2_scales, "e4m3")
    wbu = unpack_weight(wb_words, wb_scales, "e2m1")
    xtidxg = xtu[:, idx]
    xoidx2g = xou[:, idx2]
    a = wu.T @ xtidxg + w0u.T @ xoidx2g
    b = w2u.T @ xoidx2g
    pa = np.zeros((R, C))
    pa[np.arange(R)[:, None], idx3[np.arange(R) % 512 // 64]] = a
    pb = np.zeros((R, C))
    pb[np.arange(R)[:, None], idx4[np.arange(R) % 512 // 64]] = b
    pl = np.pad(pb, ((0, 0), (1, 0)))[:, :C]
    hid = np.abs(pa - pl)
    hidq = mxq(hid, 0, "e4m3")
    p = wbu.T @ hidq
    return p

@@ -1,0 +1,213 @@
+from contextlib import ExitStack
+
+import concourse.mybir as mybir
+
+FLOPS = 536870912
+
+F32 = mybir.dt.float32
+BF16 = mybir.dt.bfloat16
+I32 = mybir.dt.int32
+U32 = mybir.dt.uint32
+U16 = mybir.dt.uint16
+U8 = mybir.dt.uint8
+E4M3 = mybir.dt.float8_e4m3fn_x4
+E5M2 = mybir.dt.float8_e5m2_x4
+E2M1 = mybir.dt.float4_e2m1fn_x4
+ACT = mybir.ActivationFunctionType
+ALU = mybir.AluOpType
+
+P = 128
+PACK = 4
+QUADS = 4
+TABLE = 1024
+SLOTS = 256
+HIDDEN = 512
+BOARD = 512
+OUT = 256
+CHUNK = 128
+CHUNKS = BOARD // CHUNK
+
+
+def tile_list_laggedboards_kernel(tc, xt_words, xt_scales, xo_words, xo_scales, w_words, w_scales, w0_words,
+                                        w0_scales, w2_words, w2_scales, wb_words, wb_scales, offs, offs2, offs3,
+                                        offs4, out):
+    nc = tc.nc
+    with ExitStack() as ctx:
+        keep = ctx.enter_context(tc.tile_pool(name="keep", bufs=1))
+        psum = ctx.enter_context(tc.psum_pool(name="psum", bufs=4))
+
+        def sbuf(name, shape, dtype, tag=""):
+            return keep.tile(shape, dtype, name=name, tag=tag, align_bytes=64)
+
+        def zeroed_plane(name, width, tag=""):
+            plane = sbuf(name, [P, width], U8, tag)
+            nc.vector.memset(plane[:].bitcast(I32), 0)
+            return plane
+
+        def load_scale_rows(plane, scales):
+            for q in range(QUADS):
+                nc.sync.dma_start(out=plane[32 * q : 32 * q + 4, :].bitcast(I32),
+                                  in_=scales[0, 4 * q : 4 * q + 4, :].bitcast(I32))
+
+        def load_list(name, source):
+            offsets = keep.tile([P, SLOTS // 16], U16, name=name)
+            nc.sync.dma_start(offsets[:], source)
+            return offsets
+
+        def load_words(name, source, width, tag=""):
+            words = sbuf(name, [P, width], U32, tag)
+            nc.sync.dma_start(out=words[:].bitcast(I32), in_=source[0].rearrange("p n t -> p (n t)").bitcast(I32))
+            return words
+
+        def load_nibbles(name, source, width, tag=""):
+            words = sbuf(name, [P, 2 * width], U8, tag)
+            nc.sync.dma_start(out=words[:].bitcast(I32), in_=source[0].bitcast(I32))
+            return words
+
+        def gather(name, window, offsets, dtype):
+            picked = sbuf(name, [P, SLOTS], dtype)
+            nc.vector.tensor_copy(out=picked[:], in_=window[:].indirect(offsets[:]))
+            return picked
+
+        def deal(dealt, source):
+            nc.vector.tensor_copy(out=dealt.rearrange("p (t m) -> p t m", m=P),
+                                  in_=source.rearrange("p (m t) -> p t m", t=PACK))
+
+        def zeroed_board(name, tag=""):
+            board = sbuf(name, [P, BOARD], F32, tag)
+            nc.vector.memset(board[:].bitcast(I32), 0)
+            return board
+
+        def copy_scalar(out, in_):
+            nc.scalar.activation(out=out, in_=in_, func=ACT.Copy)
+
+        def put(name, acc, board, offsets, copy):
+            values = sbuf(name, list(acc.shape), F32)
+            copy(out=values[:], in_=acc[:])
+            nc.scalar.activation(out=board[:].indirect(offsets), in_=values[:], func=ACT.Copy)
+
+        xo_plane = zeroed_plane("xo_plane", TABLE)
+        w2_plane = zeroed_plane("w2_plane", HIDDEN)
+        notes = load_list("notes", offs2)
+        w2_rows = sbuf("w2_rows", [4, QUADS, HIDDEN // 4], I32)
+        nc.sync.dma_start(out=w2_rows[:], in_=w2_scales[0].rearrange("(q r) n -> r q n", r=4).bitcast(I32))
+        load_scale_rows(xo_plane, xo_scales)
+        xo_table = load_words("xo_table", xo_words, TABLE)
+        w2_raw = load_words("w2_raw", w2_words, HIDDEN, tag="reuse0")
+        places_b = load_list("places_b", offs4)
+
+        xt_plane = zeroed_plane("xt_plane", TABLE)
+        w_planes = zeroed_plane("w_planes", 2 * HIDDEN)
+        wb_plane = zeroed_plane("wb_plane", OUT)
+        boards_b = [zeroed_board("board_b%d" % t) for t in range(PACK)]
+        tokens = load_list("tokens", offs)
+        load_scale_rows(xt_plane, xt_scales)
+        xt_table = load_words("xt_table", xt_words, TABLE, tag="reuse2")
+        w0_raw = load_nibbles("w0_raw", w0_words, HIDDEN, tag="reuse1")
+        w_raw = load_nibbles("w_raw", w_words, HIDDEN, tag="reuse3")
+        load_scale_rows(w_planes[:, HIDDEN : 2 * HIDDEN], w0_scales)
+        load_scale_rows(w_planes[:, 0:HIDDEN], w_scales)
+        places_a = load_list("places_a", offs3)
+        wb_codes = load_nibbles("wb_codes", wb_words, OUT)
+        load_scale_rows(wb_plane, wb_scales)
+
+        for q in range(QUADS):
+            nc.vector.tensor_copy(out=w2_plane[32 * q : 32 * q + 4, :].bitcast(I32), in_=w2_rows[:, q, :])
+        w2_scale = sbuf("w2_scale", [P, HIDDEN], U8)
+        deal(w2_scale[:], w2_plane[:])
+        xo_scale = gather("xo_scale", xo_plane, notes, U8)
+        xo_codes = gather("xo_codes", xo_table, notes, U32)
+        w2_first = sbuf("w2_first", [P, P], U32)
+        nc.vector.tensor_copy(out=w2_first[:], in_=w2_raw[:, 0:HIDDEN:PACK])
+
+        def product_b(name, t, codes, first, count, copy):
+            slots = slice(first, first + count)
+            acc = psum.tile([P, count], F32, name="acc")
+            nc.tensor.matmul_mx(out=acc[:], lhsT=codes.bitcast(E4M3), lhsT_scale=w2_scale[:, t * P : (t + 1) * P],
+                                rhs=xo_codes[:, slots].bitcast(E4M3), rhs_scale=xo_scale[:, slots],
+                                start=True, stop=True)
+            put(name, acc, boards_b[t], places_b[:, first // 16 : (first + count) // 16], copy)
+
+        product_b("b0_head", 0, w2_first[:], 0, SLOTS // 2, copy_scalar)
+        product_b("b0_tail", 0, w2_first[:], SLOTS // 2, SLOTS // 2, nc.vector.tensor_copy)
+        w2_rest = sbuf("w2_rest", [P, PACK - 1, P], U32)
+        nc.vector.tensor_copy(out=w2_rest[:], in_=w2_raw[:].rearrange("p (m t) -> p t m", t=PACK)[:, 1:, :])
+        for t in range(1, PACK):
+            product_b("b%d" % t, t, w2_rest[:, t - 1, :], 0, SLOTS, nc.vector.tensor_copy)
+
+        xt_scale = gather("xt_scale", xt_plane, tokens, U8)
+        xt_codes = gather("xt_codes", xt_table, tokens, U32)
+        w_codes = sbuf("w_codes", [P, 2 * HIDDEN], U8)
+        w0_codes = sbuf("w0_codes", [P, 2 * HIDDEN], U8)
+        w_scale = sbuf("w_scale", [P, HIDDEN], U8)
+        w0_scale = sbuf("w0_scale", [P, HIDDEN], U8)
+        deal(w0_codes[:].bitcast(U16), w0_raw[:].bitcast(U16))
+        deal(w_codes[:].bitcast(U16), w_raw[:].bitcast(U16))
+        deal(w0_scale[:], w_planes[:, HIDDEN : 2 * HIDDEN])
+        deal(w_scale[:], w_planes[:, 0:HIDDEN])
+        boards_a = [zeroed_board("board_a%d" % t, tag="reuse%d" % t) for t in range(PACK)]
+
+        diffs = [[sbuf("diff%d_%d" % (pair, q), [P, 2, CHUNK], F32) for q in range(CHUNKS)] for pair in range(2)]
+        hids = [sbuf("hid%d" % q, [P, CHUNK, PACK], BF16) for q in range(CHUNKS)]
+
+        def subtract(t, q):
+            diff = diffs[t // 2][q]
+            first = q * CHUNK
+            skip = 1 if q == 0 else 0
+            nc.vector.tensor_tensor(out=diff[:, t % 2, skip:], in0=boards_a[t][:, first + skip : first + CHUNK],
+                                    in1=boards_b[t][:, first + skip - 1 : first + CHUNK - 1], op=ALU.subtract)
+            if skip:
+                nc.vector.tensor_copy(out=diff[:, t % 2, 0:1], in_=boards_a[t][:, 0:1])
+
+        def magnitude_vector(pair, q):
+            diff = diffs[pair][q][:].rearrange("p t c -> p c t")
+            nc.vector.scalar_tensor_tensor(out=hids[q][:, :, 2 * pair : 2 * pair + 2], in0=diff, scalar=-1.0,
+                                           in1=diff, op0=ALU.mult, op1=ALU.max)
+
+        def magnitude_scalar(pair, q):
+            nc.scalar.activation(out=hids[q][:, :, 2 * pair : 2 * pair + 2],
+                                 in_=diffs[pair][q][:].rearrange("p t c -> p c t"), func=ACT.Abs)
+
+        for t in range(PACK):
+            cols = slice(t * P, (t + 1) * P)
+            code_cols = slice(2 * t * P, 2 * (t + 1) * P)
+            acc = psum.tile([P, SLOTS], F32, name="acc")
+            nc.tensor.matmul_mx(out=acc[:], lhsT=w0_codes[:, code_cols].bitcast(E2M1), lhsT_scale=w0_scale[:, cols],
+                                rhs=xo_codes[:].bitcast(E4M3), rhs_scale=xo_scale[:], start=True, stop=False)
+            nc.tensor.matmul_mx(out=acc[:], lhsT=w_codes[:, code_cols].bitcast(E2M1), lhsT_scale=w_scale[:, cols],
+                                rhs=xt_codes[:].bitcast(E5M2), rhs_scale=xt_scale[:], start=False, stop=True)
+            put("a%d" % t, acc, boards_a[t], places_a[:], nc.vector.tensor_copy)
+
+        for t in range(PACK - 1):
+            for q in range(CHUNKS):
+                subtract(t, q)
+            if t == 1:
+                for q in range(CHUNKS):
+                    magnitude_vector(0, q)
+
+        order = [1, 2, 3, 0]
+        for q in order:
+            subtract(PACK - 1, q)
+        for q in order[:-1]:
+            magnitude_scalar(1, q)
+
+        def finish(q, copy):
+            codes = sbuf("hid_codes%d" % q, [P, CHUNK], U32)
+            scale = sbuf("hid_scale%d" % q, [P, CHUNK], U8)
+            nc.vector.quantize_mx(out=codes[:].bitcast(E4M3), scales=scale[:],
+                                  in_=hids[q][:].rearrange("p c t -> p (c t)"))
+            res = psum.tile([P, OUT // P, CHUNK], F32, name="res")
+            for h in range(OUT // P):
+                nc.tensor.matmul_mx(out=res[:, h, :], lhsT=wb_codes[:, 2 * h * P : 2 * (h + 1) * P].bitcast(E2M1),
+                                    lhsT_scale=wb_plane[:, h * P : (h + 1) * P], rhs=codes[:].bitcast(E4M3),
+                                    rhs_scale=scale[:], start=True, stop=True)
+            staged = sbuf("staged%d" % q, [P, OUT // P, CHUNK], F32)
+            copy(out=staged[:], in_=res[:])
+            nc.sync.dma_start(out=out.rearrange("(h p) c -> p h c", p=P)[:, :, q * CHUNK : (q + 1) * CHUNK],
+                              in_=staged[:])
+
+        finish(order[0], nc.scalar.copy)
+        magnitude_vector(1, order[-1])
+        finish(order[1], nc.scalar.copy)
+        finish(order[3], nc.vector.tensor_copy)
+        finish(order[2], nc.scalar.copy)

@@ -21,6 +21,7 @@ PACK = 4
 QUADS = 4
 TABLE = 1024
 SLOTS = 256
+HALF = SLOTS // 2
 HIDDEN = 512
 BOARD = 512
 OUT = 256
@@ -34,14 +35,15 @@ def tile_list_laggedboards_kernel(tc, xt_words, xt_scales, xo_words, xo_scales, 
     nc = tc.nc
     with ExitStack() as ctx:
         keep = ctx.enter_context(tc.tile_pool(name="keep", bufs=1))
+        early = ctx.enter_context(tc.tile_pool(name="early", bufs=1))
         psum = ctx.enter_context(tc.psum_pool(name="psum", bufs=4))
 
         def sbuf(name, shape, dtype, tag=""):
             return keep.tile(shape, dtype, name=name, tag=tag, align_bytes=64)
 
-        def zeroed_plane(name, width, tag=""):
-            plane = sbuf(name, [P, width], U8, tag)
-            nc.vector.memset(plane[:].bitcast(I32), 0)
+        def zeroed_plane(engine, name, width):
+            plane = sbuf(name, [P, width], U8)
+            engine.memset(plane[:].bitcast(I32), 0)
             return plane
 
         def load_scale_rows(plane, scales):
@@ -54,10 +56,8 @@ def tile_list_laggedboards_kernel(tc, xt_words, xt_scales, xo_words, xo_scales, 
             nc.sync.dma_start(offsets[:], source)
             return offsets
 
-        def load_words(name, source, width, tag=""):
-            words = sbuf(name, [P, width], U32, tag)
+        def load_words(words, source):
             nc.sync.dma_start(out=words[:].bitcast(I32), in_=source[0].rearrange("p n t -> p (n t)").bitcast(I32))
-            return words
 
         def load_nibbles(name, source, width, tag=""):
             words = sbuf(name, [P, 2 * width], U8, tag)
@@ -69,42 +69,48 @@ def tile_list_laggedboards_kernel(tc, xt_words, xt_scales, xo_words, xo_scales, 
             nc.vector.tensor_copy(out=picked[:], in_=window[:].indirect(offsets[:]))
             return picked
 
-        def deal(dealt, source):
+        def deal(dealt, source, first=0, last=PACK):
             nc.vector.tensor_copy(out=dealt.rearrange("p (t m) -> p t m", m=P),
-                                  in_=source.rearrange("p (m t) -> p t m", t=PACK))
+                                  in_=source.rearrange("p (m t) -> p t m", t=PACK)[:, first:last, :])
 
-        def zeroed_board(name, tag=""):
+        def zeroed_board(engine, name, tag=""):
             board = sbuf(name, [P, BOARD], F32, tag)
-            nc.vector.memset(board[:].bitcast(I32), 0)
+            engine.memset(board[:].bitcast(I32), 0)
             return board
 
         def copy_scalar(out, in_):
             nc.scalar.activation(out=out, in_=in_, func=ACT.Copy)
 
-        def put(name, acc, board, offsets, copy):
-            values = sbuf(name, list(acc.shape), F32)
+        def leave_psum(name, acc, copy, tag=""):
+            values = sbuf(name, list(acc.shape), F32, tag)
             copy(out=values[:], in_=acc[:])
-            nc.scalar.activation(out=board[:].indirect(offsets), in_=values[:], func=ACT.Copy)
+            return values
 
-        xo_plane = zeroed_plane("xo_plane", TABLE)
-        w2_plane = zeroed_plane("w2_plane", HIDDEN)
+        def put(board, offsets, values):
+            nc.scalar.activation(out=board[:].indirect(offsets), in_=values, func=ACT.Copy)
+
+        xo_plane = zeroed_plane(nc.gpsimd, "xo_plane", TABLE)
+        w2_plane = zeroed_plane(nc.vector, "w2_plane", HIDDEN)
         notes = load_list("notes", offs2)
         w2_rows = sbuf("w2_rows", [4, QUADS, HIDDEN // 4], I32)
         nc.sync.dma_start(out=w2_rows[:], in_=w2_scales[0].rearrange("(q r) n -> r q n", r=4).bitcast(I32))
+        w2_raw = sbuf("w2_raw", [P, HIDDEN], U32)
+        load_words(w2_raw, w2_words)
         load_scale_rows(xo_plane, xo_scales)
-        xo_table = load_words("xo_table", xo_words, TABLE)
-        w2_raw = load_words("w2_raw", w2_words, HIDDEN, tag="reuse0")
+        xo_table = early.tile([P, TABLE], U32, name="xo_table", align_bytes=64, offset=0)
+        load_words(xo_table, xo_words)
         places_b = load_list("places_b", offs4)
 
-        xt_plane = zeroed_plane("xt_plane", TABLE)
-        w_planes = zeroed_plane("w_planes", 2 * HIDDEN)
-        wb_plane = zeroed_plane("wb_plane", OUT)
-        boards_b = [zeroed_board("board_b%d" % t) for t in range(PACK)]
+        xt_plane = zeroed_plane(nc.vector, "xt_plane", TABLE)
+        w_planes = zeroed_plane(nc.vector, "w_planes", 2 * HIDDEN)
+        wb_plane = zeroed_plane(nc.vector, "wb_plane", OUT)
+        boards_b = [zeroed_board(nc.gpsimd, "board_b%d" % t) for t in range(2)]
         tokens = load_list("tokens", offs)
         load_scale_rows(xt_plane, xt_scales)
-        xt_table = load_words("xt_table", xt_words, TABLE, tag="reuse2")
-        w0_raw = load_nibbles("w0_raw", w0_words, HIDDEN, tag="reuse1")
-        w_raw = load_nibbles("w_raw", w_words, HIDDEN, tag="reuse3")
+        w0_raw = load_nibbles("w0_raw", w0_words, HIDDEN)
+        w_raw = load_nibbles("w_raw", w_words, HIDDEN)
+        xt_table = sbuf("xt_table", [P, TABLE], U32)
+        load_words(xt_table, xt_words)
         load_scale_rows(w_planes[:, HIDDEN : 2 * HIDDEN], w0_scales)
         load_scale_rows(w_planes[:, 0:HIDDEN], w_scales)
         places_a = load_list("places_a", offs3)
@@ -113,27 +119,43 @@ def tile_list_laggedboards_kernel(tc, xt_words, xt_scales, xo_words, xo_scales, 
 
         for q in range(QUADS):
             nc.vector.tensor_copy(out=w2_plane[32 * q : 32 * q + 4, :].bitcast(I32), in_=w2_rows[:, q, :])
-        w2_scale = sbuf("w2_scale", [P, HIDDEN], U8)
-        deal(w2_scale[:], w2_plane[:])
+        w2_early = sbuf("w2_early", [P, 2 * P], U32)
+        w2_scale_early = sbuf("w2_scale_early", [P, 2 * P], U8)
+        deal(w2_scale_early[:], w2_plane[:], 0, 2)
+        deal(w2_early[:], w2_raw[:], 0, 2)
         xo_scale = gather("xo_scale", xo_plane, notes, U8)
-        xo_codes = gather("xo_codes", xo_table, notes, U32)
-        w2_first = sbuf("w2_first", [P, P], U32)
-        nc.vector.tensor_copy(out=w2_first[:], in_=w2_raw[:, 0:HIDDEN:PACK])
+        xo_codes = sbuf("xo_codes", [P, SLOTS], U32)
+        for half in range(2):
+            nc.vector.tensor_copy(out=xo_codes[:, half * HALF : (half + 1) * HALF],
+                                  in_=xo_table[:].indirect(notes[:, half * HALF // 16 : (half + 1) * HALF // 16]))
 
-        def product_b(name, t, codes, first, count, copy):
-            slots = slice(first, first + count)
-            acc = psum.tile([P, count], F32, name="acc")
-            nc.tensor.matmul_mx(out=acc[:], lhsT=codes.bitcast(E4M3), lhsT_scale=w2_scale[:, t * P : (t + 1) * P],
-                                rhs=xo_codes[:, slots].bitcast(E4M3), rhs_scale=xo_scale[:, slots],
-                                start=True, stop=True)
-            put(name, acc, boards_b[t], places_b[:, first // 16 : (first + count) // 16], copy)
+        def product_b(acc, codes, scale, i, slots):
+            nc.tensor.matmul_mx(out=acc, lhsT=codes[:, i * P : (i + 1) * P].bitcast(E4M3),
+                                lhsT_scale=scale[:, i * P : (i + 1) * P], rhs=xo_codes[:, slots].bitcast(E4M3),
+                                rhs_scale=xo_scale[:, slots], start=True, stop=True)
 
-        product_b("b0_head", 0, w2_first[:], 0, SLOTS // 2, copy_scalar)
-        product_b("b0_tail", 0, w2_first[:], SLOTS // 2, SLOTS // 2, nc.vector.tensor_copy)
-        w2_rest = sbuf("w2_rest", [P, PACK - 1, P], U32)
-        nc.vector.tensor_copy(out=w2_rest[:], in_=w2_raw[:].rearrange("p (m t) -> p t m", t=PACK)[:, 1:, :])
-        for t in range(1, PACK):
-            product_b("b%d" % t, t, w2_rest[:, t - 1, :], 0, SLOTS, nc.vector.tensor_copy)
+        for t, copy in ((0, copy_scalar), (1, nc.vector.tensor_copy)):
+            acc = psum.tile([P, HALF], F32, name="acc")
+            product_b(acc[:], w2_early, w2_scale_early, t, slice(0, HALF))
+            values = leave_psum("b%d_head" % t, acc, copy, tag="reuse%d" % t)
+            put(boards_b[t], places_b[:, 0 : HALF // 16], values[:])
+        acc = psum.tile([P, 2, HALF], F32, name="acc")
+        for t in range(2):
+            product_b(acc[:, t, :], w2_early, w2_scale_early, t, slice(HALF, SLOTS))
+        values = leave_psum("b01_tail", acc, nc.vector.tensor_copy, tag="reuse2")
+        for t in range(2):
+            put(boards_b[t], places_b[:, HALF // 16 : SLOTS // 16], values[:, t, :])
+
+        w2_late = early.tile([P, 2 * P], U32, name="w2_late", align_bytes=64, offset=0)
+        w2_scale_late = early.tile([P, 2 * P], U8, name="w2_scale_late", align_bytes=64, offset=4 * 2 * P)
+        deal(w2_scale_late[:], w2_plane[:], 2, 4)
+        deal(w2_late[:], w2_raw[:], 2, 4)
+        for t in range(2, PACK):
+            boards_b.append(zeroed_board(nc.gpsimd, "board_b%d" % t, tag="reuse%d" % (t - 2)))
+            acc = psum.tile([P, SLOTS], F32, name="acc")
+            product_b(acc[:], w2_late, w2_scale_late, t - 2, slice(0, SLOTS))
+            values = leave_psum("b%d" % t, acc, nc.vector.tensor_copy, tag="reuse%d" % (t + 1))
+            put(boards_b[t], places_b[:], values[:])
 
         xt_scale = gather("xt_scale", xt_plane, tokens, U8)
         xt_codes = gather("xt_codes", xt_table, tokens, U32)
@@ -145,7 +167,7 @@ def tile_list_laggedboards_kernel(tc, xt_words, xt_scales, xo_words, xo_scales, 
         deal(w_codes[:].bitcast(U16), w_raw[:].bitcast(U16))
         deal(w0_scale[:], w_planes[:, HIDDEN : 2 * HIDDEN])
         deal(w_scale[:], w_planes[:, 0:HIDDEN])
-        boards_a = [zeroed_board("board_a%d" % t, tag="reuse%d" % t) for t in range(PACK)]
+        boards_a = []
 
         diffs = [[sbuf("diff%d_%d" % (pair, q), [P, 2, CHUNK], F32) for q in range(CHUNKS)] for pair in range(2)]
         hids = [sbuf("hid%d" % q, [P, CHUNK, PACK], BF16) for q in range(CHUNKS)]
@@ -171,12 +193,14 @@ def tile_list_laggedboards_kernel(tc, xt_words, xt_scales, xo_words, xo_scales, 
         for t in range(PACK):
             cols = slice(t * P, (t + 1) * P)
             code_cols = slice(2 * t * P, 2 * (t + 1) * P)
+            boards_a.append(zeroed_board(nc.gpsimd, "board_a%d" % t, tag="reuse%d" % (t + 2)))
             acc = psum.tile([P, SLOTS], F32, name="acc")
             nc.tensor.matmul_mx(out=acc[:], lhsT=w0_codes[:, code_cols].bitcast(E2M1), lhsT_scale=w0_scale[:, cols],
                                 rhs=xo_codes[:].bitcast(E4M3), rhs_scale=xo_scale[:], start=True, stop=False)
             nc.tensor.matmul_mx(out=acc[:], lhsT=w_codes[:, code_cols].bitcast(E2M1), lhsT_scale=w_scale[:, cols],
                                 rhs=xt_codes[:].bitcast(E5M2), rhs_scale=xt_scale[:], start=False, stop=True)
-            put("a%d" % t, acc, boards_a[t], places_a[:], nc.vector.tensor_copy)
+            values = leave_psum("a%d" % t, acc, nc.vector.tensor_copy, tag="reuse5" if t == 0 else "")
+            put(boards_a[t], places_a[:], values[:])
 
         for t in range(PACK - 1):
             for q in range(CHUNKS):
@@ -191,23 +215,40 @@ def tile_list_laggedboards_kernel(tc, xt_words, xt_scales, xo_words, xo_scales, 
         for q in order[:-1]:
             magnitude_scalar(1, q)
 
-        def finish(q, copy):
+        def quantise(q):
             codes = sbuf("hid_codes%d" % q, [P, CHUNK], U32)
             scale = sbuf("hid_scale%d" % q, [P, CHUNK], U8)
             nc.vector.quantize_mx(out=codes[:].bitcast(E4M3), scales=scale[:],
                                   in_=hids[q][:].rearrange("p c t -> p (c t)"))
-            res = psum.tile([P, OUT // P, CHUNK], F32, name="res")
-            for h in range(OUT // P):
-                nc.tensor.matmul_mx(out=res[:, h, :], lhsT=wb_codes[:, 2 * h * P : 2 * (h + 1) * P].bitcast(E2M1),
-                                    lhsT_scale=wb_plane[:, h * P : (h + 1) * P], rhs=codes[:].bitcast(E4M3),
-                                    rhs_scale=scale[:], start=True, stop=True)
-            staged = sbuf("staged%d" % q, [P, OUT // P, CHUNK], F32)
-            copy(out=staged[:], in_=res[:])
+            return codes, scale
+
+        def product_out(res, h, codes, scale):
+            nc.tensor.matmul_mx(out=res, lhsT=wb_codes[:, 2 * h * P : 2 * (h + 1) * P].bitcast(E2M1),
+                                lhsT_scale=wb_plane[:, h * P : (h + 1) * P], rhs=codes[:].bitcast(E4M3),
+                                rhs_scale=scale[:], start=True, stop=True)
+
+        def store(q, staged):
             nc.sync.dma_start(out=out.rearrange("(h p) c -> p h c", p=P)[:, :, q * CHUNK : (q + 1) * CHUNK],
                               in_=staged[:])
 
-        finish(order[0], nc.scalar.copy)
+        def finish(q):
+            codes, scale = quantise(q)
+            res = psum.tile([P, OUT // P, CHUNK], F32, name="res")
+            for h in range(OUT // P):
+                product_out(res[:, h, :], h, codes, scale)
+            store(q, leave_psum("staged%d" % q, res, nc.scalar.copy))
+
+        def finish_last(q):
+            codes, scale = quantise(q)
+            staged = sbuf("staged%d" % q, [P, OUT // P, CHUNK], F32)
+            for h, copy in enumerate((nc.vector.tensor_copy, nc.scalar.copy)):
+                res = psum.tile([P, CHUNK], F32, name="acc")
+                product_out(res[:], h, codes, scale)
+                copy(out=staged[:, h, :], in_=res[:])
+            store(q, staged)
+
+        finish(order[0])
         magnitude_vector(1, order[-1])
-        finish(order[1], nc.scalar.copy)
-        finish(order[3], nc.vector.tensor_copy)
-        finish(order[2], nc.scalar.copy)
+        finish(order[1])
+        finish(order[3])
+        finish_last(order[2])

@@ -51,6 +51,13 @@ def tile_list_laggedboards_kernel(tc, xt_words, xt_scales, xo_words, xo_scales, 
                 nc.sync.dma_start(out=plane[32 * q : 32 * q + 4, :].bitcast(I32),
                                   in_=scales[0, 4 * q : 4 * q + 4, :].bitcast(I32))
 
+        def stage_scale_rows(rows, scales):
+            nc.sync.dma_start(out=rows, in_=scales[0].rearrange("(q r) n -> r q n", r=4).bitcast(I32))
+
+        def spread_scale_rows(plane, rows):
+            for q in range(QUADS):
+                nc.vector.tensor_copy(out=plane[32 * q : 32 * q + 4, :].bitcast(I32), in_=rows[:, q, :])
+
         def load_list(name, source):
             offsets = keep.tile([P, SLOTS // 16], U16, name=name)
             nc.sync.dma_start(offsets[:], source)
@@ -93,7 +100,7 @@ def tile_list_laggedboards_kernel(tc, xt_words, xt_scales, xo_words, xo_scales, 
         w2_plane = zeroed_plane(nc.vector, "w2_plane", HIDDEN)
         notes = load_list("notes", offs2)
         w2_rows = sbuf("w2_rows", [4, QUADS, HIDDEN // 4], I32)
-        nc.sync.dma_start(out=w2_rows[:], in_=w2_scales[0].rearrange("(q r) n -> r q n", r=4).bitcast(I32))
+        stage_scale_rows(w2_rows[:], w2_scales)
         w2_raw = sbuf("w2_raw", [P, HIDDEN], U32)
         load_words(w2_raw, w2_words)
         load_scale_rows(xo_plane, xo_scales)
@@ -102,23 +109,22 @@ def tile_list_laggedboards_kernel(tc, xt_words, xt_scales, xo_words, xo_scales, 
         places_b = load_list("places_b", offs4)
 
         xt_plane = zeroed_plane(nc.vector, "xt_plane", TABLE)
+        boards_b = [zeroed_board(nc.gpsimd, "board_b%d" % t) for t in range(2)]
         w_planes = zeroed_plane(nc.vector, "w_planes", 2 * HIDDEN)
         wb_plane = zeroed_plane(nc.vector, "wb_plane", OUT)
-        boards_b = [zeroed_board(nc.gpsimd, "board_b%d" % t) for t in range(2)]
         tokens = load_list("tokens", offs)
         load_scale_rows(xt_plane, xt_scales)
+        xt_table = sbuf("xt_table", [P, TABLE], U32, tag="reuse4")
+        load_words(xt_table, xt_words)
         w0_raw = load_nibbles("w0_raw", w0_words, HIDDEN)
         w_raw = load_nibbles("w_raw", w_words, HIDDEN)
-        xt_table = sbuf("xt_table", [P, TABLE], U32)
-        load_words(xt_table, xt_words)
-        load_scale_rows(w_planes[:, HIDDEN : 2 * HIDDEN], w0_scales)
         load_scale_rows(w_planes[:, 0:HIDDEN], w_scales)
+        load_scale_rows(w_planes[:, HIDDEN : 2 * HIDDEN], w0_scales)
         places_a = load_list("places_a", offs3)
         wb_codes = load_nibbles("wb_codes", wb_words, OUT)
         load_scale_rows(wb_plane, wb_scales)
 
-        for q in range(QUADS):
-            nc.vector.tensor_copy(out=w2_plane[32 * q : 32 * q + 4, :].bitcast(I32), in_=w2_rows[:, q, :])
+        spread_scale_rows(w2_plane, w2_rows)
         w2_early = sbuf("w2_early", [P, 2 * P], U32)
         w2_scale_early = sbuf("w2_scale_early", [P, 2 * P], U8)
         deal(w2_scale_early[:], w2_plane[:], 0, 2)
@@ -150,23 +156,25 @@ def tile_list_laggedboards_kernel(tc, xt_words, xt_scales, xo_words, xo_scales, 
         w2_scale_late = early.tile([P, 2 * P], U8, name="w2_scale_late", align_bytes=64, offset=4 * 2 * P)
         deal(w2_scale_late[:], w2_plane[:], 2, 4)
         deal(w2_late[:], w2_raw[:], 2, 4)
+        late_values = []
         for t in range(2, PACK):
-            boards_b.append(zeroed_board(nc.gpsimd, "board_b%d" % t, tag="reuse%d" % (t - 2)))
             acc = psum.tile([P, SLOTS], F32, name="acc")
             product_b(acc[:], w2_late, w2_scale_late, t - 2, slice(0, SLOTS))
-            values = leave_psum("b%d" % t, acc, nc.vector.tensor_copy, tag="reuse%d" % (t + 1))
-            put(boards_b[t], places_b[:], values[:])
+            late_values.append(leave_psum("b%d" % t, acc, nc.vector.tensor_copy, tag="reuse3" if t == 2 else ""))
+        boards_b.append(zeroed_board(nc.gpsimd, "board_b2", tag="reuse0"))
+        put(boards_b[2], places_b[:], late_values[0][:])
 
         xt_scale = gather("xt_scale", xt_plane, tokens, U8)
         xt_codes = gather("xt_codes", xt_table, tokens, U32)
         w_codes = sbuf("w_codes", [P, 2 * HIDDEN], U8)
         w0_codes = sbuf("w0_codes", [P, 2 * HIDDEN], U8)
-        w_scale = sbuf("w_scale", [P, HIDDEN], U8)
-        w0_scale = sbuf("w0_scale", [P, HIDDEN], U8)
+        scale_first = sbuf("scale_first", [P, 2, P], U8)
+        scale_rest = sbuf("scale_rest", [P, 2, PACK - 1, P], U8)
         deal(w0_codes[:].bitcast(U16), w0_raw[:].bitcast(U16))
         deal(w_codes[:].bitcast(U16), w_raw[:].bitcast(U16))
-        deal(w0_scale[:], w_planes[:, HIDDEN : 2 * HIDDEN])
-        deal(w_scale[:], w_planes[:, 0:HIDDEN])
+        by_tile = w_planes[:].rearrange("p (i m t) -> p i t m", i=2, t=PACK)
+        nc.vector.tensor_copy(out=scale_first[:], in_=by_tile[:, :, 0, :])
+        nc.vector.tensor_copy(out=scale_rest[:], in_=by_tile[:, :, 1:, :])
         boards_a = []
 
         diffs = [[sbuf("diff%d_%d" % (pair, q), [P, 2, CHUNK], F32) for q in range(CHUNKS)] for pair in range(2)]
@@ -191,16 +199,18 @@ def tile_list_laggedboards_kernel(tc, xt_words, xt_scales, xo_words, xo_scales, 
                                  in_=diffs[pair][q][:].rearrange("p t c -> p c t"), func=ACT.Abs)
 
         for t in range(PACK):
-            cols = slice(t * P, (t + 1) * P)
+            scale = scale_first[:] if t == 0 else scale_rest[:, :, t - 1, :]
             code_cols = slice(2 * t * P, 2 * (t + 1) * P)
-            boards_a.append(zeroed_board(nc.gpsimd, "board_a%d" % t, tag="reuse%d" % (t + 2)))
+            boards_a.append(zeroed_board(nc.gpsimd, "board_a%d" % t, tag="reuse%d" % (t + 1)))
             acc = psum.tile([P, SLOTS], F32, name="acc")
-            nc.tensor.matmul_mx(out=acc[:], lhsT=w0_codes[:, code_cols].bitcast(E2M1), lhsT_scale=w0_scale[:, cols],
+            nc.tensor.matmul_mx(out=acc[:], lhsT=w0_codes[:, code_cols].bitcast(E2M1), lhsT_scale=scale[:, 1, :],
                                 rhs=xo_codes[:].bitcast(E4M3), rhs_scale=xo_scale[:], start=True, stop=False)
-            nc.tensor.matmul_mx(out=acc[:], lhsT=w_codes[:, code_cols].bitcast(E2M1), lhsT_scale=w_scale[:, cols],
+            nc.tensor.matmul_mx(out=acc[:], lhsT=w_codes[:, code_cols].bitcast(E2M1), lhsT_scale=scale[:, 0, :],
                                 rhs=xt_codes[:].bitcast(E5M2), rhs_scale=xt_scale[:], start=False, stop=True)
-            values = leave_psum("a%d" % t, acc, nc.vector.tensor_copy, tag="reuse5" if t == 0 else "")
+            values = leave_psum("a%d" % t, acc, nc.vector.tensor_copy, tag="reuse5" if t == 1 else "")
             put(boards_a[t], places_a[:], values[:])
+        boards_b.append(zeroed_board(nc.gpsimd, "board_b3", tag="reuse5"))
+        put(boards_b[3], places_b[:], late_values[1][:])
 
         for t in range(PACK - 1):
             for q in range(CHUNKS):

@@ -21,7 +21,7 @@ PACK = 4
 QUADS = 4
 TABLE = 1024
 SLOTS = 256
-HALF = SLOTS // 2
+HEAD = 64
 HIDDEN = 512
 BOARD = 512
 OUT = 256
@@ -109,7 +109,7 @@ def tile_list_laggedboards_kernel(tc, xt_words, xt_scales, xo_words, xo_scales, 
         places_b = load_list("places_b", offs4)
 
         xt_plane = zeroed_plane(nc.vector, "xt_plane", TABLE)
-        boards_b = [zeroed_board(nc.gpsimd, "board_b%d" % t) for t in range(2)]
+        boards_b = [zeroed_board(nc.vector, "board_b%d" % t) for t in range(2)]
         w_planes = zeroed_plane(nc.vector, "w_planes", 2 * HIDDEN)
         wb_plane = zeroed_plane(nc.vector, "wb_plane", OUT)
         tokens = load_list("tokens", offs)
@@ -131,9 +131,9 @@ def tile_list_laggedboards_kernel(tc, xt_words, xt_scales, xo_words, xo_scales, 
         deal(w2_early[:], w2_raw[:], 0, 2)
         xo_scale = gather("xo_scale", xo_plane, notes, U8)
         xo_codes = sbuf("xo_codes", [P, SLOTS], U32)
-        for half in range(2):
-            nc.vector.tensor_copy(out=xo_codes[:, half * HALF : (half + 1) * HALF],
-                                  in_=xo_table[:].indirect(notes[:, half * HALF // 16 : (half + 1) * HALF // 16]))
+        for first, last in ((0, HEAD), (HEAD, SLOTS)):
+            nc.vector.tensor_copy(out=xo_codes[:, first:last],
+                                  in_=xo_table[:].indirect(notes[:, first // 16 : last // 16]))
 
         def product_b(acc, codes, scale, i, slots):
             nc.tensor.matmul_mx(out=acc, lhsT=codes[:, i * P : (i + 1) * P].bitcast(E4M3),
@@ -141,16 +141,16 @@ def tile_list_laggedboards_kernel(tc, xt_words, xt_scales, xo_words, xo_scales, 
                                 rhs_scale=xo_scale[:, slots], start=True, stop=True)
 
         for t, copy in ((0, copy_scalar), (1, nc.vector.tensor_copy)):
-            acc = psum.tile([P, HALF], F32, name="acc")
-            product_b(acc[:], w2_early, w2_scale_early, t, slice(0, HALF))
+            acc = psum.tile([P, HEAD], F32, name="acc")
+            product_b(acc[:], w2_early, w2_scale_early, t, slice(0, HEAD))
             values = leave_psum("b%d_head" % t, acc, copy, tag="reuse%d" % t)
-            put(boards_b[t], places_b[:, 0 : HALF // 16], values[:])
-        acc = psum.tile([P, 2, HALF], F32, name="acc")
+            put(boards_b[t], places_b[:, 0 : HEAD // 16], values[:])
         for t in range(2):
-            product_b(acc[:, t, :], w2_early, w2_scale_early, t, slice(HALF, SLOTS))
-        values = leave_psum("b01_tail", acc, nc.vector.tensor_copy, tag="reuse2")
-        for t in range(2):
-            put(boards_b[t], places_b[:, HALF // 16 : SLOTS // 16], values[:, t, :])
+            acc = psum.tile([P, SLOTS - HEAD], F32, name="acc")
+            product_b(acc[:, 0:HEAD], w2_early, w2_scale_early, t, slice(HEAD, 2 * HEAD))
+            product_b(acc[:, HEAD:], w2_early, w2_scale_early, t, slice(2 * HEAD, SLOTS))
+            values = leave_psum("b%d_tail" % t, acc, nc.vector.tensor_copy, tag="reuse2" if t == 0 else "")
+            put(boards_b[t], places_b[:, HEAD // 16 : SLOTS // 16], values[:])
 
         w2_late = early.tile([P, 2 * P], U32, name="w2_late", align_bytes=64, offset=0)
         w2_scale_late = early.tile([P, 2 * P], U8, name="w2_scale_late", align_bytes=64, offset=4 * 2 * P)

from contextlib import ExitStack

import concourse.mybir as mybir

FLOPS = 536870912

F32 = mybir.dt.float32
BF16 = mybir.dt.bfloat16
I32 = mybir.dt.int32
U32 = mybir.dt.uint32
U16 = mybir.dt.uint16
U8 = mybir.dt.uint8
E4M3 = mybir.dt.float8_e4m3fn_x4
E5M2 = mybir.dt.float8_e5m2_x4
E2M1 = mybir.dt.float4_e2m1fn_x4
ACT = mybir.ActivationFunctionType
ALU = mybir.AluOpType

P = 128
PACK = 4
QUADS = 4
TABLE = 1024
SLOTS = 256
HEAD = 64
HIDDEN = 512
BOARD = 512
OUT = 256
CHUNK = 128
CHUNKS = BOARD // CHUNK


def tile_list_laggedboards_kernel(tc, xt_words, xt_scales, xo_words, xo_scales, w_words, w_scales, w0_words,
                                        w0_scales, w2_words, w2_scales, wb_words, wb_scales, offs, offs2, offs3,
                                        offs4, out):
    nc = tc.nc
    with ExitStack() as ctx:
        keep = ctx.enter_context(tc.tile_pool(name="keep", bufs=1))
        early = ctx.enter_context(tc.tile_pool(name="early", bufs=1))
        psum = ctx.enter_context(tc.psum_pool(name="psum", bufs=4))

        def sbuf(name, shape, dtype, tag=""):
            return keep.tile(shape, dtype, name=name, tag=tag, align_bytes=64)

        def zeroed_plane(engine, name, width):
            plane = sbuf(name, [P, width], U8)
            engine.memset(plane[:].bitcast(I32), 0)
            return plane

        def load_scale_rows(plane, scales):
            for q in range(QUADS):
                nc.sync.dma_start(out=plane[32 * q : 32 * q + 4, :].bitcast(I32),
                                  in_=scales[0, 4 * q : 4 * q + 4, :].bitcast(I32))

        def stage_scale_rows(rows, scales):
            nc.sync.dma_start(out=rows, in_=scales[0].rearrange("(q r) n -> r q n", r=4).bitcast(I32))

        def spread_scale_rows(plane, rows):
            for q in range(QUADS):
                nc.vector.tensor_copy(out=plane[32 * q : 32 * q + 4, :].bitcast(I32), in_=rows[:, q, :])

        def load_list(name, source):
            offsets = keep.tile([P, SLOTS // 16], U16, name=name)
            nc.sync.dma_start(offsets[:], source)
            return offsets

        def load_words(words, source):
            nc.sync.dma_start(out=words[:].bitcast(I32), in_=source[0].rearrange("p n t -> p (n t)").bitcast(I32))

        def load_nibbles(name, source, width, tag=""):
            words = sbuf(name, [P, 2 * width], U8, tag)
            nc.sync.dma_start(out=words[:].bitcast(I32), in_=source[0].bitcast(I32))
            return words

        def gather(name, window, offsets, dtype):
            picked = sbuf(name, [P, SLOTS], dtype)
            nc.vector.tensor_copy(out=picked[:], in_=window[:].indirect(offsets[:]))
            return picked

        def deal(dealt, source, first=0, last=PACK):
            nc.vector.tensor_copy(out=dealt.rearrange("p (t m) -> p t m", m=P),
                                  in_=source.rearrange("p (m t) -> p t m", t=PACK)[:, first:last, :])

        def zeroed_board(engine, name, tag=""):
            board = sbuf(name, [P, BOARD], F32, tag)
            engine.memset(board[:].bitcast(I32), 0)
            return board

        def copy_scalar(out, in_):
            nc.scalar.activation(out=out, in_=in_, func=ACT.Copy)

        def leave_psum(name, acc, copy, tag=""):
            values = sbuf(name, list(acc.shape), F32, tag)
            copy(out=values[:], in_=acc[:])
            return values

        def put(board, offsets, values):
            nc.scalar.activation(out=board[:].indirect(offsets), in_=values, func=ACT.Copy)

        xo_plane = zeroed_plane(nc.gpsimd, "xo_plane", TABLE)
        w2_plane = zeroed_plane(nc.vector, "w2_plane", HIDDEN)
        notes = load_list("notes", offs2)
        w2_rows = sbuf("w2_rows", [4, QUADS, HIDDEN // 4], I32)
        stage_scale_rows(w2_rows[:], w2_scales)
        w2_raw = sbuf("w2_raw", [P, HIDDEN], U32)
        load_words(w2_raw, w2_words)
        load_scale_rows(xo_plane, xo_scales)
        xo_table = early.tile([P, TABLE], U32, name="xo_table", align_bytes=64, offset=0)
        load_words(xo_table, xo_words)
        places_b = load_list("places_b", offs4)

        xt_plane = zeroed_plane(nc.vector, "xt_plane", TABLE)
        boards_b = [zeroed_board(nc.vector, "board_b%d" % t) for t in range(2)]
        w_planes = zeroed_plane(nc.vector, "w_planes", 2 * HIDDEN)
        wb_plane = zeroed_plane(nc.vector, "wb_plane", OUT)
        tokens = load_list("tokens", offs)
        load_scale_rows(xt_plane, xt_scales)
        xt_table = sbuf("xt_table", [P, TABLE], U32, tag="reuse4")
        load_words(xt_table, xt_words)
        w0_raw = load_nibbles("w0_raw", w0_words, HIDDEN)
        w_raw = load_nibbles("w_raw", w_words, HIDDEN)
        load_scale_rows(w_planes[:, 0:HIDDEN], w_scales)
        load_scale_rows(w_planes[:, HIDDEN : 2 * HIDDEN], w0_scales)
        places_a = load_list("places_a", offs3)
        wb_codes = load_nibbles("wb_codes", wb_words, OUT)
        load_scale_rows(wb_plane, wb_scales)

        spread_scale_rows(w2_plane, w2_rows)
        w2_early = sbuf("w2_early", [P, 2 * P], U32)
        w2_scale_early = sbuf("w2_scale_early", [P, 2 * P], U8)
        deal(w2_scale_early[:], w2_plane[:], 0, 2)
        deal(w2_early[:], w2_raw[:], 0, 2)
        xo_scale = gather("xo_scale", xo_plane, notes, U8)
        xo_codes = sbuf("xo_codes", [P, SLOTS], U32)
        for first, last in ((0, HEAD), (HEAD, SLOTS)):
            nc.vector.tensor_copy(out=xo_codes[:, first:last],
                                  in_=xo_table[:].indirect(notes[:, first // 16 : last // 16]))

        def product_b(acc, codes, scale, i, slots):
            nc.tensor.matmul_mx(out=acc, lhsT=codes[:, i * P : (i + 1) * P].bitcast(E4M3),
                                lhsT_scale=scale[:, i * P : (i + 1) * P], rhs=xo_codes[:, slots].bitcast(E4M3),
                                rhs_scale=xo_scale[:, slots], start=True, stop=True)

        for t, copy in ((0, copy_scalar), (1, nc.vector.tensor_copy)):
            acc = psum.tile([P, HEAD], F32, name="acc")
            product_b(acc[:], w2_early, w2_scale_early, t, slice(0, HEAD))
            values = leave_psum("b%d_head" % t, acc, copy, tag="reuse%d" % t)
            put(boards_b[t], places_b[:, 0 : HEAD // 16], values[:])
        for t in range(2):
            acc = psum.tile([P, SLOTS - HEAD], F32, name="acc")
            product_b(acc[:, 0:HEAD], w2_early, w2_scale_early, t, slice(HEAD, 2 * HEAD))
            product_b(acc[:, HEAD:], w2_early, w2_scale_early, t, slice(2 * HEAD, SLOTS))
            values = leave_psum("b%d_tail" % t, acc, nc.vector.tensor_copy, tag="reuse2" if t == 0 else "")
            put(boards_b[t], places_b[:, HEAD // 16 : SLOTS // 16], values[:])

        w2_late = early.tile([P, 2 * P], U32, name="w2_late", align_bytes=64, offset=0)
        w2_scale_late = early.tile([P, 2 * P], U8, name="w2_scale_late", align_bytes=64, offset=4 * 2 * P)
        deal(w2_scale_late[:], w2_plane[:], 2, 4)
        deal(w2_late[:], w2_raw[:], 2, 4)
        late_values = []
        for t in range(2, PACK):
            acc = psum.tile([P, SLOTS], F32, name="acc")
            product_b(acc[:], w2_late, w2_scale_late, t - 2, slice(0, SLOTS))
            late_values.append(leave_psum("b%d" % t, acc, nc.vector.tensor_copy, tag="reuse3" if t == 2 else ""))
        boards_b.append(zeroed_board(nc.gpsimd, "board_b2", tag="reuse0"))
        put(boards_b[2], places_b[:], late_values[0][:])

        xt_scale = gather("xt_scale", xt_plane, tokens, U8)
        xt_codes = gather("xt_codes", xt_table, tokens, U32)
        w_codes = sbuf("w_codes", [P, 2 * HIDDEN], U8)
        w0_codes = sbuf("w0_codes", [P, 2 * HIDDEN], U8)
        scale_first = sbuf("scale_first", [P, 2, P], U8)
        scale_rest = sbuf("scale_rest", [P, 2, PACK - 1, P], U8)
        deal(w0_codes[:].bitcast(U16), w0_raw[:].bitcast(U16))
        deal(w_codes[:].bitcast(U16), w_raw[:].bitcast(U16))
        by_tile = w_planes[:].rearrange("p (i m t) -> p i t m", i=2, t=PACK)
        nc.vector.tensor_copy(out=scale_first[:], in_=by_tile[:, :, 0, :])
        nc.vector.tensor_copy(out=scale_rest[:], in_=by_tile[:, :, 1:, :])
        boards_a = []

        diffs = [[sbuf("diff%d_%d" % (pair, q), [P, 2, CHUNK], F32) for q in range(CHUNKS)] for pair in range(2)]
        hids = [sbuf("hid%d" % q, [P, CHUNK, PACK], BF16) for q in range(CHUNKS)]

        def subtract(t, q):
            diff = diffs[t // 2][q]
            first = q * CHUNK
            skip = 1 if q == 0 else 0
            nc.vector.tensor_tensor(out=diff[:, t % 2, skip:], in0=boards_a[t][:, first + skip : first + CHUNK],
                                    in1=boards_b[t][:, first + skip - 1 : first + CHUNK - 1], op=ALU.subtract)
            if skip:
                nc.vector.tensor_copy(out=diff[:, t % 2, 0:1], in_=boards_a[t][:, 0:1])

        def magnitude_vector(pair, q):
            diff = diffs[pair][q][:].rearrange("p t c -> p c t")
            nc.vector.scalar_tensor_tensor(out=hids[q][:, :, 2 * pair : 2 * pair + 2], in0=diff, scalar=-1.0,
                                           in1=diff, op0=ALU.mult, op1=ALU.max)

        def magnitude_scalar(pair, q):
            nc.scalar.activation(out=hids[q][:, :, 2 * pair : 2 * pair + 2],
                                 in_=diffs[pair][q][:].rearrange("p t c -> p c t"), func=ACT.Abs)

        for t in range(PACK):
            scale = scale_first[:] if t == 0 else scale_rest[:, :, t - 1, :]
            code_cols = slice(2 * t * P, 2 * (t + 1) * P)
            boards_a.append(zeroed_board(nc.gpsimd, "board_a%d" % t, tag="reuse%d" % (t + 1)))
            acc = psum.tile([P, SLOTS], F32, name="acc")
            nc.tensor.matmul_mx(out=acc[:], lhsT=w0_codes[:, code_cols].bitcast(E2M1), lhsT_scale=scale[:, 1, :],
                                rhs=xo_codes[:].bitcast(E4M3), rhs_scale=xo_scale[:], start=True, stop=False)
            nc.tensor.matmul_mx(out=acc[:], lhsT=w_codes[:, code_cols].bitcast(E2M1), lhsT_scale=scale[:, 0, :],
                                rhs=xt_codes[:].bitcast(E5M2), rhs_scale=xt_scale[:], start=False, stop=True)
            values = leave_psum("a%d" % t, acc, nc.vector.tensor_copy, tag="reuse5" if t == 1 else "")
            put(boards_a[t], places_a[:], values[:])
        boards_b.append(zeroed_board(nc.gpsimd, "board_b3", tag="reuse5"))
        put(boards_b[3], places_b[:], late_values[1][:])

        for t in range(PACK - 1):
            for q in range(CHUNKS):
                subtract(t, q)
            if t == 1:
                for q in range(CHUNKS):
                    magnitude_vector(0, q)

        order = [1, 2, 3, 0]
        for q in order:
            subtract(PACK - 1, q)
        for q in order[:-1]:
            magnitude_scalar(1, q)

        def quantise(q):
            codes = sbuf("hid_codes%d" % q, [P, CHUNK], U32)
            scale = sbuf("hid_scale%d" % q, [P, CHUNK], U8)
            nc.vector.quantize_mx(out=codes[:].bitcast(E4M3), scales=scale[:],
                                  in_=hids[q][:].rearrange("p c t -> p (c t)"))
            return codes, scale

        def product_out(res, h, codes, scale):
            nc.tensor.matmul_mx(out=res, lhsT=wb_codes[:, 2 * h * P : 2 * (h + 1) * P].bitcast(E2M1),
                                lhsT_scale=wb_plane[:, h * P : (h + 1) * P], rhs=codes[:].bitcast(E4M3),
                                rhs_scale=scale[:], start=True, stop=True)

        def store(q, staged):
            nc.sync.dma_start(out=out.rearrange("(h p) c -> p h c", p=P)[:, :, q * CHUNK : (q + 1) * CHUNK],
                              in_=staged[:])

        def finish(q):
            codes, scale = quantise(q)
            res = psum.tile([P, OUT // P, CHUNK], F32, name="res")
            for h in range(OUT // P):
                product_out(res[:, h, :], h, codes, scale)
            store(q, leave_psum("staged%d" % q, res, nc.scalar.copy))

        def finish_last(q):
            codes, scale = quantise(q)
            staged = sbuf("staged%d" % q, [P, OUT // P, CHUNK], F32)
            for h, copy in enumerate((nc.vector.tensor_copy, nc.scalar.copy)):
                res = psum.tile([P, CHUNK], F32, name="acc")
                product_out(res[:], h, codes, scale)
                copy(out=staged[:, h, :], in_=res[:])
            store(q, staged)

        finish(order[0])
        magnitude_vector(1, order[-1])
        finish(order[1])
        finish(order[3])
        finish_last(order[2])
